import numpy as np
import ml_dtypes


def mxq(x, axis, fmt="e4m3"):
    dtype, down = {"e4m3": (ml_dtypes.float8_e4m3fn, 7), "e5m2": (ml_dtypes.float8_e5m2, 14)}[fmt]
    v = np.moveaxis(np.asarray(x, np.float32).astype(ml_dtypes.bfloat16).astype(np.float64), axis, -1)
    blocks = v.reshape(v.shape[:-1] + (-1, 32))
    amax = np.abs(blocks).max(-1, keepdims=True)
    byte = np.maximum(np.where(amax > 0, np.frexp(amax)[1] - 1 + 127, 0) - down, 1)
    scale = np.exp2(byte - 127.0)
    codes = (blocks / scale).astype(np.float32).astype(dtype).astype(np.float64)
    return np.moveaxis((codes * scale).reshape(v.shape), -1, axis)


WIDE = False


def mx_kscale(k):
    if not WIDE:
        return np.ones(k)
    levels = np.array([10, -10, 5, -5, 0])
    if k % 512:
        return np.exp2(np.random.permutation(np.resize(levels, k // 32))).repeat(32)
    a = np.empty((k // 512, 16))
    for p in range(k // 512):
        a[p, :8] = np.random.permutation(np.resize(levels, 8))
        for g in range(8):
            far = levels[np.abs(levels - a[p, g]) >= 10]
            a[p, g + 8] = far[np.random.randint(len(far))]
    return np.exp2(a.ravel()).repeat(32)


def f64(x):
    return np.asarray(x).astype(np.float64)


def striped8(idx):
    return np.concatenate([x.reshape(-1, 16).T for x in idx]).astype(np.uint16)


def runs(offs, k):
    lists = np.stack([offs[16 * r : 16 * r + 16].T.reshape(-1) for r in range(8)]).astype(np.int64)
    return lists[np.arange(k) % 512 // 64]


def pack_weight(w):
    k, n = w.shape
    w = f64(np.asarray(w, np.float32).astype(ml_dtypes.bfloat16)).reshape(k // 32, 32, n)
    amax = np.abs(w).max(1)
    byte = np.clip(np.where(amax > 0, np.frexp(amax)[1] - 1 + 127 - 7, 1), 1, 254)
    scaled = (w * np.exp2(127.0 - byte)[:, None, :]).reshape(k, n).astype(np.float32)
    words = np.ascontiguousarray(scaled.reshape(k // 512, 128, 4, n).transpose(0, 1, 3, 2)).astype(ml_dtypes.float8_e4m3fn).view(np.uint8)
    return words, np.ascontiguousarray(byte.astype(np.uint8).reshape(k // 512, 16, n))


def unpack_weight(words, scales):
    g, p, n, _ = words.shape
    vals = np.ascontiguousarray(words).view(ml_dtypes.float8_e4m3fn).astype(np.float64) * np.repeat(np.exp2(scales.astype(np.float64) - 127.0), 8, axis=1)[..., None]
    return vals.transpose(0, 1, 3, 2).reshape(g * 512, n)


K, T, S, V, N, H = 512, 2048, 512, 256, 512, 512


def setup_inputs():
    n = np.random.standard_normal
    s = mx_kscale(K)[:, None]
    u = mx_kscale(H)
    packed_xT = pack_weight(n((K, T)) * s)
    perm = np.stack([np.random.permutation(S) for _ in range(8)])
    return {
        "x_words": packed_xT[0],
        "x_scales": packed_xT[1],
        "w1": (n((K, H)) / np.sqrt(K) / s).astype(np.float32),
        "gn": (np.random.uniform(0.5, 1.5, (H, 1)) * u[:, None]).astype(np.float32),
        "w2": (n((H, N)) / np.sqrt(H) / u[:, None]).astype(np.float32),
        "offs": striped8(np.random.randint(0, T, (8, S))),
        "la": striped8(perm[:, :V]),
        "lb": striped8(perm[:, V:]),
    }


def reference(x_words, x_scales, w1, gn, w2, offs, la, lb):
    xq = unpack_weight(x_words, x_scales)[np.arange(K)[:, None], runs(offs, K)]
    y = mxq(f64(w1), 0, "e4m3").T @ xq
    a = y[np.arange(H)[:, None], runs(la, H)]
    b = y[np.arange(H)[:, None], runs(lb, H)]
    rt_n = np.sqrt((a) ** 2 + (b) ** 2 + 0.25)
    nb = (a * b) / rt_n
    d1 = np.zeros((H, S))
    d1[np.arange(H)[:, None], runs(la, H)] = rt_n
    d2 = d1.copy()
    d2[np.arange(H)[:, None], runs(lb, H)] = nb
    z = f64(gn) * d2
    return mxq(f64(w2), 0, "e4m3").T @ mxq(z, 0, "e4m3")

@@ -1,0 +1,174 @@
+from contextlib import ExitStack
+
+import concourse.mybir as mybir
+
+K, T, S, V, H, N = 512, 2048, 512, 256, 512, 512
+FLOPS = 2 * K * H * S + 2 * H * N * S
+
+F32 = mybir.dt.float32
+BF16 = mybir.dt.bfloat16
+I32 = mybir.dt.int32
+U32 = mybir.dt.uint32
+U16 = mybir.dt.uint16
+U8 = mybir.dt.uint8
+FP8X4 = mybir.dt.float8_e4m3fn_x4
+ACT = mybir.ActivationFunctionType
+ALU = mybir.AluOpType
+
+P = 128
+PACK = 4
+HALF = 256
+ORDER = (2, 0, 1, 3)
+
+
+def tile_picked_hashpolar_none_p_kernel(tc, x_words, x_scales, w1, gn, w2, offs, la, lb, out):
+    nc = tc.nc
+    with ExitStack() as ctx:
+        lists = ctx.enter_context(tc.tile_pool(name="lists", bufs=1))
+        keep = ctx.enter_context(tc.tile_pool(name="keep", bufs=1))
+        stage = ctx.enter_context(tc.tile_pool(name="stage", bufs=1))
+        psum = ctx.enter_context(tc.psum_pool(name="psum", bufs=8))
+
+        offs_sb = lists.tile([P, S // 16], U16, name="offs_sb")
+        la_sb = lists.tile([P, V // 16], U16, name="la_sb")
+        lb_sb = lists.tile([P, V // 16], U16, name="lb_sb")
+        nc.sync.dma_start(offs_sb[:], offs)
+
+        table_scales = keep.tile([P, T], U8, name="table_scales", align_bytes=64)
+        scale_rows = x_scales[0].bitcast(I32)
+        nc.sync.dma_start(table_scales[:].bitcast(I32), scale_rows.unsqueeze(1).to_broadcast([16, 8, T // 4]))
+
+        table_words = keep.tile([P, T], I32, name="table_words", align_bytes=64)
+        nc.sync.dma_start(table_words[:], x_words[0].rearrange("p n t -> p (n t)").bitcast(I32))
+
+        w1_rows = w1.rearrange("(p j) c -> p j c", j=PACK)
+        w1_raw = []
+        for h in range(2):
+            raw = stage.tile([P, PACK, HALF], F32, name=f"w_raw{h}", tag=f"w_raw{h}")
+            nc.sync.dma_start(raw[:], w1_rows[:, :, h * HALF : (h + 1) * HALF])
+            w1_raw.append(raw)
+        nc.sync.dma_start(la_sb[:], la)
+        nc.sync.dma_start(lb_sb[:], lb)
+
+        gain = keep.tile([P, PACK], F32, name="gain")
+        nc.gpsimd.dma_start(gain[:], gn.rearrange("(p t) o -> p (t o)", t=PACK))
+
+        warm = keep.tile([P, 1], F32, name="warm")
+        warm_out = keep.tile([P, 1], F32, name="warm_out")
+        nc.vector.memset(warm[:], 1.0)
+        nc.scalar.activation(warm_out[:], warm[:], ACT.Abs_reciprocal_sqrt)
+
+        picked_scales = keep.tile([P, S], U8, name="picked_scales", align_bytes=64)
+        nc.vector.tensor_copy(picked_scales[:], table_scales[:].indirect(offs_sb[:]))
+        x_plane = keep.tile([P, S], U8, name="x_plane", align_bytes=64)
+        nc.vector.tensor_copy(x_plane[:].bitcast(I32), picked_scales[:].bitcast(I32))
+        for i in range(1, 4):
+            nc.scalar.dma_start(x_plane[:].bitcast(I32)[i:P:32, :], picked_scales[:].bitcast(I32)[8 * i : P : 32, :])
+        x_codes = keep.tile([P, S], U32, name="x_codes", align_bytes=64)
+        nc.vector.tensor_copy(x_codes[:], table_words[:].bitcast(U32).indirect(offs_sb[:]))
+
+        w1_bf = [keep.tile([P, P, PACK], BF16, name=f"w1_bf{t}", align_bytes=64) for t in range(PACK)]
+        for h in range(2):
+            dealt = w1_raw[h][:].rearrange("p j (m t) -> p t m j", t=PACK)
+            for t in ORDER:
+                dst = w1_bf[t][:, h * 64 : (h + 1) * 64, :]
+                if h == 0 or t in ORDER[2:]:
+                    nc.scalar.copy(dst, dealt[:, t, :, :])
+                else:
+                    nc.vector.tensor_copy(dst, dealt[:, t, :, :])
+        y_sb = {}
+        for t in ORDER:
+            codes = keep.tile([P, P], U32, name=f"w1_codes{t}", align_bytes=64)
+            plane = keep.tile([P, P], U8, name=f"w1_plane{t}", align_bytes=64)
+            nc.vector.quantize_mx(out=codes[:].bitcast(FP8X4), scales=plane[:], in_=w1_bf[t][:].rearrange("p m j -> p (m j)"))
+            y = keep.tile([P, S], F32, name=f"y{t}")
+            pieces = 2 if t == ORDER[0] else 1
+            for g in range(pieces):
+                cols = slice(g * S // pieces, (g + 1) * S // pieces)
+                acc = psum.tile([P, S // pieces], F32, name="acc", tag="acc")
+                nc.tensor.matmul_mx(out=acc[:], lhsT=codes[:].bitcast(FP8X4), lhsT_scale=plane[:], rhs=x_codes[:, cols].bitcast(FP8X4), rhs_scale=x_plane[:, cols], start=True, stop=True)
+                if g == 0:
+                    nc.scalar.copy(y[:, cols], acc[:])
+                else:
+                    nc.vector.tensor_copy(y[:, cols], acc[:])
+            y_sb[t] = y
+
+        w2_rows = w2.rearrange("(p j) c -> p j c", j=PACK)
+        w2_bf = keep.tile([P, N, PACK], BF16, name="w2_bf", align_bytes=64)
+        for h in range(2):
+            raw = stage.tile([P, PACK, HALF], F32, name=f"w_raw{h}", tag=f"w_raw{h}")
+            nc.sync.dma_start(raw[:], w2_rows[:, :, h * HALF : (h + 1) * HALF])
+            for q in range(2):
+                c0 = h * HALF + q * P
+                nc.scalar.copy(w2_bf[:, c0 : c0 + P, :].rearrange("p (c i) j -> p c j i", i=4), raw[:, :, q * P : (q + 1) * P].rearrange("p j (c i) -> p c j i", i=4))
+        w2_codes = keep.tile([P, N], U32, name="w2_codes", align_bytes=64)
+        w2_plane = keep.tile([P, N], U8, name="w2_plane", align_bytes=64)
+        nc.vector.quantize_mx(out=w2_codes[:].bitcast(FP8X4), scales=w2_plane[:], in_=w2_bf[:].rearrange("p c j -> p (c j)"))
+
+        z_bf = [keep.tile([P, P, PACK], BF16, name=f"z_bf{q}", align_bytes=64) for q in range(4)]
+        sums, prods, invs, pairs = {}, {}, {}, {}
+        for b in range(2):
+            batch = ORDER[2 * b : 2 * b + 2]
+            pair = keep.tile([P, 2, 2, V], F32, name=f"pair{b}")
+            sq = keep.tile([P, 2, 2, V], F32, name=f"sq{b}")
+            for i, t in enumerate(batch):
+                nc.vector.tensor_copy(pair[:, i, 0, :], y_sb[t][:].indirect(la_sb[:]))
+                nc.vector.tensor_copy(pair[:, i, 1, :], y_sb[t][:].indirect(lb_sb[:]))
+                nc.scalar.activation(sq[:, i, :, :], pair[:, i, :, :], ACT.Square)
+                pairs[t] = pair[:, i, :, :]
+            n_now = 2 - b
+            prod = keep.tile([P, n_now, V], F32, name=f"prod{b}")
+            nc.vector.tensor_tensor(prod[:], pair[:, :n_now, 0, :], pair[:, :n_now, 1, :], ALU.mult)
+            ssum = keep.tile([P, 2, V], F32, name=f"ssum{b}")
+            nc.vector.scalar_tensor_tensor(ssum[:], sq[:, :, 0, :], 0.25, sq[:, :, 1, :], ALU.add, ALU.add)
+            inv = keep.tile([P, 2, V], F32, name=f"inv{b}")
+            nc.scalar.activation(inv[:], ssum[:], ACT.Abs_reciprocal_sqrt)
+            for i, t in enumerate(batch):
+                sums[t], invs[t] = ssum[:, i, :], inv[:, i, :]
+                if i < n_now:
+                    prods[t] = prod[:, i, :]
+
+        placed = {}
+        for b in range(2):
+            batch = ORDER[2 * b : 2 * b + 2]
+            for t in batch:
+                placed[t] = keep.tile([P, S], F32, name=f"placed{t}", tag=f"placed{t}")
+                nc.vector.tensor_tensor(placed[t][:].indirect(la_sb[:]), sums[t], invs[t], ALU.mult)
+                if t == ORDER[2]:
+                    late = keep.tile([P, V], F32, name="late", tag=f"placed{ORDER[0]}")
+                    nc.vector.tensor_tensor(late[:], pairs[ORDER[3]][:, 0, :], pairs[ORDER[3]][:, 1, :], ALU.mult)
+                    prods[ORDER[3]] = late[:]
+            for t in batch:
+                nc.vector.tensor_tensor(placed[t][:].indirect(lb_sb[:]), prods[t], invs[t], ALU.mult)
+                if t != ORDER[-1]:
+                    for q in range(4):
+                        nc.scalar.activation(z_bf[q][:, :, t], placed[t][:, q * P : (q + 1) * P], ACT.Copy, scale=gain[:, t : t + 1])
+
+        last = ORDER[-1]
+
+        def round_last(q):
+            nc.vector.tensor_scalar(z_bf[q][:, :, last], placed[last][:, q * P : (q + 1) * P], gain[:, last : last + 1], None, ALU.mult)
+
+        def project(q):
+            z_codes = keep.tile([P, P], U32, name=f"z_codes{q}", align_bytes=64)
+            z_plane = keep.tile([P, P], U8, name=f"z_plane{q}", align_bytes=64)
+            nc.vector.quantize_mx(out=z_codes[:].bitcast(FP8X4), scales=z_plane[:], in_=z_bf[q][:].rearrange("p c j -> p (c j)"))
+            groups = ((0, 4),) if q < 3 else ((0, 2), (2, 4))
+            for lo, hi in groups:
+                acc = psum.tile([P, hi - lo, P], F32, name="acc", tag="acc")
+                for a in range(lo, hi):
+                    m = slice(a * P, (a + 1) * P)
+                    nc.tensor.matmul_mx(out=acc[:, a - lo, :], lhsT=w2_codes[:, m].bitcast(FP8X4), lhsT_scale=w2_plane[:, m], rhs=z_codes[:].bitcast(FP8X4), rhs_scale=z_plane[:], start=True, stop=True)
+                res = keep.tile([P, hi - lo, P], F32, name=f"res{q}{lo}")
+                if q == 2 or lo == 2:
+                    nc.vector.tensor_copy(res[:], acc[:])
+                else:
+                    nc.scalar.copy(res[:], acc[:])
+                rows = out[lo * P : hi * P, q * P : (q + 1) * P].rearrange("(a p) c -> p a c", p=P)
+                nc.sync.dma_start(rows, res[:])
+
+        round_last(0)
+        for q in range(4):
+            if q < 3:
+                round_last(q + 1)
+            project(q)

@@ -18,7 +18,8 @@ ALU = mybir.AluOpType
 P = 128
 PACK = 4
 HALF = 256
-ORDER = (2, 0, 1, 3)
+ORDER = (1, 2, 3, 0)
+W1_VECTOR_SHARE = 40
 
 
 def tile_picked_hashpolar_none_p_kernel(tc, x_words, x_scales, w1, gn, w2, offs, la, lb, out):
@@ -27,6 +28,7 @@ def tile_picked_hashpolar_none_p_kernel(tc, x_words, x_scales, w1, gn, w2, offs,
         lists = ctx.enter_context(tc.tile_pool(name="lists", bufs=1))
         keep = ctx.enter_context(tc.tile_pool(name="keep", bufs=1))
         stage = ctx.enter_context(tc.tile_pool(name="stage", bufs=1))
+        shared = ctx.enter_context(tc.tile_pool(name="shared", bufs=1))
         psum = ctx.enter_context(tc.psum_pool(name="psum", bufs=8))
 
         offs_sb = lists.tile([P, S // 16], U16, name="offs_sb")
@@ -67,31 +69,63 @@ def tile_picked_hashpolar_none_p_kernel(tc, x_words, x_scales, w1, gn, w2, offs,
         x_codes = keep.tile([P, S], U32, name="x_codes", align_bytes=64)
         nc.vector.tensor_copy(x_codes[:], table_words[:].bitcast(U32).indirect(offs_sb[:]))
 
-        w1_bf = [keep.tile([P, P, PACK], BF16, name=f"w1_bf{t}", align_bytes=64) for t in range(PACK)]
+        w1_bf = keep.tile([P, PACK, P, PACK], BF16, name="w1_bf", align_bytes=64)
         for h in range(2):
-            dealt = w1_raw[h][:].rearrange("p j (m t) -> p t m j", t=PACK)
-            for t in ORDER:
-                dst = w1_bf[t][:, h * 64 : (h + 1) * 64, :]
-                if h == 0 or t in ORDER[2:]:
-                    nc.scalar.copy(dst, dealt[:, t, :, :])
-                else:
-                    nc.vector.tensor_copy(dst, dealt[:, t, :, :])
+            src = w1_raw[h][:].rearrange("p j (m t) -> p m j t", t=PACK)
+            dst = w1_bf[:, :, h * 64 : (h + 1) * 64, :].rearrange("p t m j -> p m j t")
+            nc.vector.tensor_copy(dst[:, :W1_VECTOR_SHARE, :, :], src[:, :W1_VECTOR_SHARE, :, :])
+            nc.scalar.copy(dst[:, W1_VECTOR_SHARE:, :, :], src[:, W1_VECTOR_SHARE:, :, :])
+        w1_mx = {}
+        for lo, hi in ((1, 2), (2, 4), (0, 1)):
+            codes = keep.tile([P, hi - lo, P], U32, name=f"w1_codes{lo}", align_bytes=64)
+            plane = keep.tile([P, hi - lo, P], U8, name=f"w1_plane{lo}", align_bytes=64)
+            nc.vector.quantize_mx(
+                out=codes[:].rearrange("p t m -> p (t m)").bitcast(FP8X4),
+                scales=plane[:].rearrange("p t m -> p (t m)"),
+                in_=w1_bf[:, lo:hi, :, :].rearrange("p t m j -> p (t m j)"),
+            )
+            for t in range(lo, hi):
+                w1_mx[t] = codes[:, t - lo, :], plane[:, t - lo, :]
         y_sb = {}
         for t in ORDER:
-            codes = keep.tile([P, P], U32, name=f"w1_codes{t}", align_bytes=64)
-            plane = keep.tile([P, P], U8, name=f"w1_plane{t}", align_bytes=64)
-            nc.vector.quantize_mx(out=codes[:].bitcast(FP8X4), scales=plane[:], in_=w1_bf[t][:].rearrange("p m j -> p (m j)"))
+            codes, plane = w1_mx[t]
             y = keep.tile([P, S], F32, name=f"y{t}")
             pieces = 2 if t == ORDER[0] else 1
             for g in range(pieces):
                 cols = slice(g * S // pieces, (g + 1) * S // pieces)
                 acc = psum.tile([P, S // pieces], F32, name="acc", tag="acc")
-                nc.tensor.matmul_mx(out=acc[:], lhsT=codes[:].bitcast(FP8X4), lhsT_scale=plane[:], rhs=x_codes[:, cols].bitcast(FP8X4), rhs_scale=x_plane[:, cols], start=True, stop=True)
+                nc.tensor.matmul_mx(out=acc[:], lhsT=codes.bitcast(FP8X4), lhsT_scale=plane, rhs=x_codes[:, cols].bitcast(FP8X4), rhs_scale=x_plane[:, cols], start=True, stop=True)
                 if g == 0:
                     nc.scalar.copy(y[:, cols], acc[:])
                 else:
                     nc.vector.tensor_copy(y[:, cols], acc[:])
             y_sb[t] = y
+
+        z_bf = [keep.tile([P, P, PACK], BF16, name=f"z_bf{q}", align_bytes=64) for q in range(4)]
+        sums, prods, invs, pairs = {}, {}, {}, {}
+        squares = []
+        for b in range(2):
+            batch = ORDER[2 * b : 2 * b + 2]
+            pair = keep.tile([P, 2, 2, V], F32, name=f"pair{b}")
+            sq = shared.tile([P, 2, 2, V], F32, name=f"sq{b}", offset=(1 - b) * 4096)
+            for i, t in enumerate(batch):
+                nc.vector.tensor_copy(pair[:, i, 0, :], y_sb[t][:].indirect(la_sb[:]))
+                nc.vector.tensor_copy(pair[:, i, 1, :], y_sb[t][:].indirect(lb_sb[:]))
+                nc.scalar.activation(sq[:, i, :, :], pair[:, i, :, :], ACT.Square)
+                pairs[t] = pair[:, i, :, :]
+            n_now = 2 - b
+            prod = keep.tile([P, n_now, V], F32, name=f"prod{b}")
+            nc.vector.tensor_tensor(prod[:], pair[:, :n_now, 0, :], pair[:, :n_now, 1, :], ALU.mult)
+            for i in range(n_now):
+                prods[batch[i]] = prod[:, i, :]
+            squares.append(sq)
+        for b in range(2):
+            ssum = keep.tile([P, 2, V], F32, name=f"ssum{b}")
+            nc.vector.scalar_tensor_tensor(ssum[:], squares[b][:, :, 0, :], 0.25, squares[b][:, :, 1, :], ALU.add, ALU.add)
+            inv = keep.tile([P, 2, V], F32, name=f"inv{b}")
+            nc.scalar.activation(inv[:], ssum[:], ACT.Abs_reciprocal_sqrt)
+            for i, t in enumerate(ORDER[2 * b : 2 * b + 2]):
+                sums[t], invs[t] = ssum[:, i, :], inv[:, i, :]
 
         w2_rows = w2.rearrange("(p j) c -> p j c", j=PACK)
         w2_bf = keep.tile([P, N, PACK], BF16, name="w2_bf", align_bytes=64)
@@ -105,37 +139,14 @@ def tile_picked_hashpolar_none_p_kernel(tc, x_words, x_scales, w1, gn, w2, offs,
         w2_plane = keep.tile([P, N], U8, name="w2_plane", align_bytes=64)
         nc.vector.quantize_mx(out=w2_codes[:].bitcast(FP8X4), scales=w2_plane[:], in_=w2_bf[:].rearrange("p c j -> p (c j)"))
 
-        z_bf = [keep.tile([P, P, PACK], BF16, name=f"z_bf{q}", align_bytes=64) for q in range(4)]
-        sums, prods, invs, pairs = {}, {}, {}, {}
-        for b in range(2):
-            batch = ORDER[2 * b : 2 * b + 2]
-            pair = keep.tile([P, 2, 2, V], F32, name=f"pair{b}")
-            sq = keep.tile([P, 2, 2, V], F32, name=f"sq{b}")
-            for i, t in enumerate(batch):
-                nc.vector.tensor_copy(pair[:, i, 0, :], y_sb[t][:].indirect(la_sb[:]))
-                nc.vector.tensor_copy(pair[:, i, 1, :], y_sb[t][:].indirect(lb_sb[:]))
-                nc.scalar.activation(sq[:, i, :, :], pair[:, i, :, :], ACT.Square)
-                pairs[t] = pair[:, i, :, :]
-            n_now = 2 - b
-            prod = keep.tile([P, n_now, V], F32, name=f"prod{b}")
-            nc.vector.tensor_tensor(prod[:], pair[:, :n_now, 0, :], pair[:, :n_now, 1, :], ALU.mult)
-            ssum = keep.tile([P, 2, V], F32, name=f"ssum{b}")
-            nc.vector.scalar_tensor_tensor(ssum[:], sq[:, :, 0, :], 0.25, sq[:, :, 1, :], ALU.add, ALU.add)
-            inv = keep.tile([P, 2, V], F32, name=f"inv{b}")
-            nc.scalar.activation(inv[:], ssum[:], ACT.Abs_reciprocal_sqrt)
-            for i, t in enumerate(batch):
-                sums[t], invs[t] = ssum[:, i, :], inv[:, i, :]
-                if i < n_now:
-                    prods[t] = prod[:, i, :]
-
         placed = {}
         for b in range(2):
             batch = ORDER[2 * b : 2 * b + 2]
             for t in batch:
-                placed[t] = keep.tile([P, S], F32, name=f"placed{t}", tag=f"placed{t}")
+                placed[t] = shared.tile([P, S], F32, name=f"placed{t}", offset=ORDER.index(t) * 2048)
                 nc.vector.tensor_tensor(placed[t][:].indirect(la_sb[:]), sums[t], invs[t], ALU.mult)
                 if t == ORDER[2]:
-                    late = keep.tile([P, V], F32, name="late", tag=f"placed{ORDER[0]}")
+                    late = shared.tile([P, V], F32, name="late", offset=0)
                     nc.vector.tensor_tensor(late[:], pairs[ORDER[3]][:, 0, :], pairs[ORDER[3]][:, 1, :], ALU.mult)
                     prods[ORDER[3]] = late[:]
             for t in batch:

@@ -1,6 +1,7 @@
 from contextlib import ExitStack
 
 import concourse.mybir as mybir
+from concourse.masks import make_identity
 
 K, T, S, V, H, N = 512, 2048, 512, 256, 512, 512
 FLOPS = 2 * K * H * S + 2 * H * N * S
@@ -28,8 +29,8 @@ def tile_picked_hashpolar_none_p_kernel(tc, x_words, x_scales, w1, gn, w2, offs,
         lists = ctx.enter_context(tc.tile_pool(name="lists", bufs=1))
         keep = ctx.enter_context(tc.tile_pool(name="keep", bufs=1))
         stage = ctx.enter_context(tc.tile_pool(name="stage", bufs=1))
-        shared = ctx.enter_context(tc.tile_pool(name="shared", bufs=1))
-        psum = ctx.enter_context(tc.psum_pool(name="psum", bufs=8))
+        psum = ctx.enter_context(tc.psum_pool(name="psum", bufs=6))
+        psum_turned = ctx.enter_context(tc.psum_pool(name="psum_turned", bufs=2))
 
         offs_sb = lists.tile([P, S // 16], U16, name="offs_sb")
         la_sb = lists.tile([P, V // 16], U16, name="la_sb")
@@ -59,6 +60,9 @@ def tile_picked_hashpolar_none_p_kernel(tc, x_words, x_scales, w1, gn, w2, offs,
         warm_out = keep.tile([P, 1], F32, name="warm_out")
         nc.vector.memset(warm[:], 1.0)
         nc.scalar.activation(warm_out[:], warm[:], ACT.Abs_reciprocal_sqrt)
+
+        ident = keep.tile([P, P], F32, name="ident")
+        make_identity(nc, ident[:])
 
         picked_scales = keep.tile([P, S], U8, name="picked_scales", align_bytes=64)
         nc.vector.tensor_copy(picked_scales[:], table_scales[:].indirect(offs_sb[:]))
@@ -102,55 +106,56 @@ def tile_picked_hashpolar_none_p_kernel(tc, x_words, x_scales, w1, gn, w2, offs,
             y_sb[t] = y
 
         z_bf = [keep.tile([P, P, PACK], BF16, name=f"z_bf{q}", align_bytes=64) for q in range(4)]
-        sums, prods, invs, pairs = {}, {}, {}, {}
-        squares = []
+        prods, invs, totals = [], [], []
         for b in range(2):
             batch = ORDER[2 * b : 2 * b + 2]
             pair = keep.tile([P, 2, 2, V], F32, name=f"pair{b}")
-            sq = shared.tile([P, 2, 2, V], F32, name=f"sq{b}", offset=(1 - b) * 4096)
+            total = psum.tile([P, 2, V], F32, name="acc", tag="acc")
             for i, t in enumerate(batch):
-                nc.vector.tensor_copy(pair[:, i, 0, :], y_sb[t][:].indirect(la_sb[:]))
-                nc.vector.tensor_copy(pair[:, i, 1, :], y_sb[t][:].indirect(lb_sb[:]))
-                nc.scalar.activation(sq[:, i, :, :], pair[:, i, :, :], ACT.Square)
-                pairs[t] = pair[:, i, :, :]
-            n_now = 2 - b
-            prod = keep.tile([P, n_now, V], F32, name=f"prod{b}")
-            nc.vector.tensor_tensor(prod[:], pair[:, :n_now, 0, :], pair[:, :n_now, 1, :], ALU.mult)
-            for i in range(n_now):
-                prods[batch[i]] = prod[:, i, :]
-            squares.append(sq)
-        for b in range(2):
-            ssum = keep.tile([P, 2, V], F32, name=f"ssum{b}")
-            nc.vector.scalar_tensor_tensor(ssum[:], squares[b][:, :, 0, :], 0.25, squares[b][:, :, 1, :], ALU.add, ALU.add)
+                turned = psum_turned.tile([P, 2, 2, P], F32, name="turned", tag="turned")
+                for side, entries in enumerate((la_sb, lb_sb)):
+                    nc.vector.tensor_copy(pair[:, i, side, :], y_sb[t][:].indirect(entries[:]))
+                    for g in range(2):
+                        nc.tensor.transpose(turned[:, side, g, :], pair[:, i, side, g * P : (g + 1) * P], ident[:])
+                sq = keep.tile([P, 2, 2, P], F32, name=f"sq{t}")
+                nc.scalar.activation(sq[:], turned[:], ACT.Square)
+                for g in range(2):
+                    for side in range(2):
+                        nc.tensor.matmul(total[:, i, g * P : (g + 1) * P], sq[:, side, g, :], ident[:], is_transpose=True, start=(side == 0), stop=(side == 1))
+            prod = keep.tile([P, 2, V], F32, name=f"prod{b}")
+            nc.vector.tensor_tensor(prod[:], pair[:, :, 0, :], pair[:, :, 1, :], ALU.mult)
             inv = keep.tile([P, 2, V], F32, name=f"inv{b}")
-            nc.scalar.activation(inv[:], ssum[:], ACT.Abs_reciprocal_sqrt)
-            for i, t in enumerate(ORDER[2 * b : 2 * b + 2]):
-                sums[t], invs[t] = ssum[:, i, :], inv[:, i, :]
+            nc.scalar.activation(inv[:], total[:], ACT.Abs_reciprocal_sqrt, bias=0.25)
+            prods.append(prod)
+            invs.append(inv)
+            totals.append(total)
 
-        w2_rows = w2.rearrange("(p j) c -> p j c", j=PACK)
-        w2_bf = keep.tile([P, N, PACK], BF16, name="w2_bf", align_bytes=64)
-        for h in range(2):
-            raw = stage.tile([P, PACK, HALF], F32, name=f"w_raw{h}", tag=f"w_raw{h}")
-            nc.sync.dma_start(raw[:], w2_rows[:, :, h * HALF : (h + 1) * HALF])
-            for q in range(2):
-                c0 = h * HALF + q * P
-                nc.scalar.copy(w2_bf[:, c0 : c0 + P, :].rearrange("p (c i) j -> p c j i", i=4), raw[:, :, q * P : (q + 1) * P].rearrange("p j (c i) -> p c j i", i=4))
         w2_codes = keep.tile([P, N], U32, name="w2_codes", align_bytes=64)
         w2_plane = keep.tile([P, N], U8, name="w2_plane", align_bytes=64)
-        nc.vector.quantize_mx(out=w2_codes[:].bitcast(FP8X4), scales=w2_plane[:], in_=w2_bf[:].rearrange("p c j -> p (c j)"))
+
+        def convert_w2():
+            w2_rows = w2.rearrange("(p j) c -> p j c", j=PACK)
+            w2_bf = keep.tile([P, N, PACK], BF16, name="w2_bf", align_bytes=64)
+            for h in range(2):
+                raw = stage.tile([P, PACK, HALF], F32, name=f"w_raw{h}", tag=f"w_raw{h}")
+                nc.sync.dma_start(raw[:], w2_rows[:, :, h * HALF : (h + 1) * HALF])
+                for q in range(2):
+                    c0 = h * HALF + q * P
+                    nc.scalar.copy(w2_bf[:, c0 : c0 + P, :].rearrange("p (c i) j -> p c j i", i=4), raw[:, :, q * P : (q + 1) * P].rearrange("p j (c i) -> p c j i", i=4))
+            nc.vector.quantize_mx(out=w2_codes[:].bitcast(FP8X4), scales=w2_plane[:], in_=w2_bf[:].rearrange("p c j -> p (c j)"))
 
         placed = {}
         for b in range(2):
             batch = ORDER[2 * b : 2 * b + 2]
-            for t in batch:
-                placed[t] = shared.tile([P, S], F32, name=f"placed{t}", offset=ORDER.index(t) * 2048)
-                nc.vector.tensor_tensor(placed[t][:].indirect(la_sb[:]), sums[t], invs[t], ALU.mult)
-                if t == ORDER[2]:
-                    late = shared.tile([P, V], F32, name="late", offset=0)
-                    nc.vector.tensor_tensor(late[:], pairs[ORDER[3]][:, 0, :], pairs[ORDER[3]][:, 1, :], ALU.mult)
-                    prods[ORDER[3]] = late[:]
-            for t in batch:
-                nc.vector.tensor_tensor(placed[t][:].indirect(lb_sb[:]), prods[t], invs[t], ALU.mult)
+            ssum = keep.tile([P, 2, V], F32, name=f"ssum{b}", tag="ssum" if b == 0 else f"placed{ORDER[0]}")
+            nc.scalar.activation(ssum[:], totals[b][:], ACT.Copy, bias=0.25)
+            if b == 0:
+                convert_w2()
+            for i, t in enumerate(batch):
+                placed[t] = keep.tile([P, S], F32, name=f"placed{t}", tag=f"placed{t}")
+                nc.vector.tensor_tensor(placed[t][:].indirect(lb_sb[:]), prods[b][:, i, :], invs[b][:, i, :], ALU.mult)
+            for i, t in enumerate(batch):
+                nc.vector.tensor_tensor(placed[t][:].indirect(la_sb[:]), ssum[:, i, :], invs[b][:, i, :], ALU.mult)
                 if t != ORDER[-1]:
                     for q in range(4):
                         nc.scalar.activation(z_bf[q][:, :, t], placed[t][:, q * P : (q + 1) * P], ACT.Copy, scale=gain[:, t : t + 1])
@@ -164,14 +169,14 @@ def tile_picked_hashpolar_none_p_kernel(tc, x_words, x_scales, w1, gn, w2, offs,
             z_codes = keep.tile([P, P], U32, name=f"z_codes{q}", align_bytes=64)
             z_plane = keep.tile([P, P], U8, name=f"z_plane{q}", align_bytes=64)
             nc.vector.quantize_mx(out=z_codes[:].bitcast(FP8X4), scales=z_plane[:], in_=z_bf[q][:].rearrange("p c j -> p (c j)"))
-            groups = ((0, 4),) if q < 3 else ((0, 2), (2, 4))
+            groups = ((0, 4),) if q in (1, 2) else ((0, 2), (2, 4))
             for lo, hi in groups:
                 acc = psum.tile([P, hi - lo, P], F32, name="acc", tag="acc")
                 for a in range(lo, hi):
                     m = slice(a * P, (a + 1) * P)
                     nc.tensor.matmul_mx(out=acc[:, a - lo, :], lhsT=w2_codes[:, m].bitcast(FP8X4), lhsT_scale=w2_plane[:, m], rhs=z_codes[:].bitcast(FP8X4), rhs_scale=z_plane[:], start=True, stop=True)
                 res = keep.tile([P, hi - lo, P], F32, name=f"res{q}{lo}")
-                if q == 2 or lo == 2:
+                if q == 2 or (q == 3 and lo == 2):
                     nc.vector.tensor_copy(res[:], acc[:])
                 else:
                     nc.scalar.copy(res[:], acc[:])

@@ -35,11 +35,11 @@ def tile_picked_hashpolar_none_p_kernel(tc, x_words, x_scales, w1, gn, w2, offs,
         offs_sb = lists.tile([P, S // 16], U16, name="offs_sb")
         la_sb = lists.tile([P, V // 16], U16, name="la_sb")
         lb_sb = lists.tile([P, V // 16], U16, name="lb_sb")
-        nc.sync.dma_start(offs_sb[:], offs)
 
         table_scales = keep.tile([P, T], U8, name="table_scales", align_bytes=64)
         scale_rows = x_scales[0].bitcast(I32)
         nc.sync.dma_start(table_scales[:].bitcast(I32), scale_rows.unsqueeze(1).to_broadcast([16, 8, T // 4]))
+        nc.sync.dma_start(offs_sb[:], offs)
 
         table_words = keep.tile([P, T], I32, name="table_words", align_bytes=64)
         nc.sync.dma_start(table_words[:], x_words[0].rearrange("p n t -> p (n t)").bitcast(I32))
@@ -123,7 +123,9 @@ def tile_picked_hashpolar_none_p_kernel(tc, x_words, x_scales, w1, gn, w2, offs,
                     for side in range(2):
                         nc.tensor.matmul(total[:, i, g * P : (g + 1) * P], sq[:, side, g, :], ident[:], is_transpose=True, start=(side == 0), stop=(side == 1))
             prod = keep.tile([P, 2, V], F32, name=f"prod{b}")
-            nc.vector.tensor_tensor(prod[:], pair[:, :, 0, :], pair[:, :, 1, :], ALU.mult)
+            for i, t in enumerate(batch):
+                engine = nc.vector if t == ORDER[-1] else nc.gpsimd
+                engine.tensor_tensor(prod[:, i, :], pair[:, i, 0, :], pair[:, i, 1, :], ALU.mult)
             inv = keep.tile([P, 2, V], F32, name=f"inv{b}")
             nc.scalar.activation(inv[:], total[:], ACT.Abs_reciprocal_sqrt, bias=0.25)
             prods.append(prod)

from contextlib import ExitStack

import concourse.mybir as mybir
from concourse.masks import make_identity

K, T, S, V, H, N = 512, 2048, 512, 256, 512, 512
FLOPS = 2 * K * H * S + 2 * H * N * S

F32 = mybir.dt.float32
BF16 = mybir.dt.bfloat16
I32 = mybir.dt.int32
U32 = mybir.dt.uint32
U16 = mybir.dt.uint16
U8 = mybir.dt.uint8
FP8X4 = mybir.dt.float8_e4m3fn_x4
ACT = mybir.ActivationFunctionType
ALU = mybir.AluOpType

P = 128
PACK = 4
HALF = 256
ORDER = (1, 2, 3, 0)
W1_VECTOR_SHARE = 40


def tile_picked_hashpolar_none_p_kernel(tc, x_words, x_scales, w1, gn, w2, offs, la, lb, out):
    nc = tc.nc
    with ExitStack() as ctx:
        lists = ctx.enter_context(tc.tile_pool(name="lists", bufs=1))
        keep = ctx.enter_context(tc.tile_pool(name="keep", bufs=1))
        stage = ctx.enter_context(tc.tile_pool(name="stage", bufs=1))
        psum = ctx.enter_context(tc.psum_pool(name="psum", bufs=6))
        psum_turned = ctx.enter_context(tc.psum_pool(name="psum_turned", bufs=2))

        offs_sb = lists.tile([P, S // 16], U16, name="offs_sb")
        la_sb = lists.tile([P, V // 16], U16, name="la_sb")
        lb_sb = lists.tile([P, V // 16], U16, name="lb_sb")

        table_scales = keep.tile([P, T], U8, name="table_scales", align_bytes=64)
        scale_rows = x_scales[0].bitcast(I32)
        nc.sync.dma_start(table_scales[:].bitcast(I32), scale_rows.unsqueeze(1).to_broadcast([16, 8, T // 4]))
        nc.sync.dma_start(offs_sb[:], offs)

        table_words = keep.tile([P, T], I32, name="table_words", align_bytes=64)
        nc.sync.dma_start(table_words[:], x_words[0].rearrange("p n t -> p (n t)").bitcast(I32))

        w1_rows = w1.rearrange("(p j) c -> p j c", j=PACK)
        w1_raw = []
        for h in range(2):
            raw = stage.tile([P, PACK, HALF], F32, name=f"w_raw{h}", tag=f"w_raw{h}")
            nc.sync.dma_start(raw[:], w1_rows[:, :, h * HALF : (h + 1) * HALF])
            w1_raw.append(raw)
        nc.sync.dma_start(la_sb[:], la)
        nc.sync.dma_start(lb_sb[:], lb)

        gain = keep.tile([P, PACK], F32, name="gain")
        nc.gpsimd.dma_start(gain[:], gn.rearrange("(p t) o -> p (t o)", t=PACK))

        warm = keep.tile([P, 1], F32, name="warm")
        warm_out = keep.tile([P, 1], F32, name="warm_out")
        nc.vector.memset(warm[:], 1.0)
        nc.scalar.activation(warm_out[:], warm[:], ACT.Abs_reciprocal_sqrt)

        ident = keep.tile([P, P], F32, name="ident")
        make_identity(nc, ident[:])

        picked_scales = keep.tile([P, S], U8, name="picked_scales", align_bytes=64)
        nc.vector.tensor_copy(picked_scales[:], table_scales[:].indirect(offs_sb[:]))
        x_plane = keep.tile([P, S], U8, name="x_plane", align_bytes=64)
        nc.vector.tensor_copy(x_plane[:].bitcast(I32), picked_scales[:].bitcast(I32))
        for i in range(1, 4):
            nc.scalar.dma_start(x_plane[:].bitcast(I32)[i:P:32, :], picked_scales[:].bitcast(I32)[8 * i : P : 32, :])
        x_codes = keep.tile([P, S], U32, name="x_codes", align_bytes=64)
        nc.vector.tensor_copy(x_codes[:], table_words[:].bitcast(U32).indirect(offs_sb[:]))

        w1_bf = keep.tile([P, PACK, P, PACK], BF16, name="w1_bf", align_bytes=64)
        for h in range(2):
            src = w1_raw[h][:].rearrange("p j (m t) -> p m j t", t=PACK)
            dst = w1_bf[:, :, h * 64 : (h + 1) * 64, :].rearrange("p t m j -> p m j t")
            nc.vector.tensor_copy(dst[:, :W1_VECTOR_SHARE, :, :], src[:, :W1_VECTOR_SHARE, :, :])
            nc.scalar.copy(dst[:, W1_VECTOR_SHARE:, :, :], src[:, W1_VECTOR_SHARE:, :, :])
        w1_mx = {}
        for lo, hi in ((1, 2), (2, 4), (0, 1)):
            codes = keep.tile([P, hi - lo, P], U32, name=f"w1_codes{lo}", align_bytes=64)
            plane = keep.tile([P, hi - lo, P], U8, name=f"w1_plane{lo}", align_bytes=64)
            nc.vector.quantize_mx(
                out=codes[:].rearrange("p t m -> p (t m)").bitcast(FP8X4),
                scales=plane[:].rearrange("p t m -> p (t m)"),
                in_=w1_bf[:, lo:hi, :, :].rearrange("p t m j -> p (t m j)"),
            )
            for t in range(lo, hi):
                w1_mx[t] = codes[:, t - lo, :], plane[:, t - lo, :]
        y_sb = {}
        for t in ORDER:
            codes, plane = w1_mx[t]
            y = keep.tile([P, S], F32, name=f"y{t}")
            pieces = 2 if t == ORDER[0] else 1
            for g in range(pieces):
                cols = slice(g * S // pieces, (g + 1) * S // pieces)
                acc = psum.tile([P, S // pieces], F32, name="acc", tag="acc")
                nc.tensor.matmul_mx(out=acc[:], lhsT=codes.bitcast(FP8X4), lhsT_scale=plane, rhs=x_codes[:, cols].bitcast(FP8X4), rhs_scale=x_plane[:, cols], start=True, stop=True)
                if g == 0:
                    nc.scalar.copy(y[:, cols], acc[:])
                else:
                    nc.vector.tensor_copy(y[:, cols], acc[:])
            y_sb[t] = y

        z_bf = [keep.tile([P, P, PACK], BF16, name=f"z_bf{q}", align_bytes=64) for q in range(4)]
        prods, invs, totals = [], [], []
        for b in range(2):
            batch = ORDER[2 * b : 2 * b + 2]
            pair = keep.tile([P, 2, 2, V], F32, name=f"pair{b}")
            total = psum.tile([P, 2, V], F32, name="acc", tag="acc")
            for i, t in enumerate(batch):
                turned = psum_turned.tile([P, 2, 2, P], F32, name="turned", tag="turned")
                for side, entries in enumerate((la_sb, lb_sb)):
                    nc.vector.tensor_copy(pair[:, i, side, :], y_sb[t][:].indirect(entries[:]))
                    for g in range(2):
                        nc.tensor.transpose(turned[:, side, g, :], pair[:, i, side, g * P : (g + 1) * P], ident[:])
                sq = keep.tile([P, 2, 2, P], F32, name=f"sq{t}")
                nc.scalar.activation(sq[:], turned[:], ACT.Square)
                for g in range(2):
                    for side in range(2):
                        nc.tensor.matmul(total[:, i, g * P : (g + 1) * P], sq[:, side, g, :], ident[:], is_transpose=True, start=(side == 0), stop=(side == 1))
            prod = keep.tile([P, 2, V], F32, name=f"prod{b}")
            for i, t in enumerate(batch):
                engine = nc.vector if t == ORDER[-1] else nc.gpsimd
                engine.tensor_tensor(prod[:, i, :], pair[:, i, 0, :], pair[:, i, 1, :], ALU.mult)
            inv = keep.tile([P, 2, V], F32, name=f"inv{b}")
            nc.scalar.activation(inv[:], total[:], ACT.Abs_reciprocal_sqrt, bias=0.25)
            prods.append(prod)
            invs.append(inv)
            totals.append(total)

        w2_codes = keep.tile([P, N], U32, name="w2_codes", align_bytes=64)
        w2_plane = keep.tile([P, N], U8, name="w2_plane", align_bytes=64)

        def convert_w2():
            w2_rows = w2.rearrange("(p j) c -> p j c", j=PACK)
            w2_bf = keep.tile([P, N, PACK], BF16, name="w2_bf", align_bytes=64)
            for h in range(2):
                raw = stage.tile([P, PACK, HALF], F32, name=f"w_raw{h}", tag=f"w_raw{h}")
                nc.sync.dma_start(raw[:], w2_rows[:, :, h * HALF : (h + 1) * HALF])
                for q in range(2):
                    c0 = h * HALF + q * P
                    nc.scalar.copy(w2_bf[:, c0 : c0 + P, :].rearrange("p (c i) j -> p c j i", i=4), raw[:, :, q * P : (q + 1) * P].rearrange("p j (c i) -> p c j i", i=4))
            nc.vector.quantize_mx(out=w2_codes[:].bitcast(FP8X4), scales=w2_plane[:], in_=w2_bf[:].rearrange("p c j -> p (c j)"))

        placed = {}
        for b in range(2):
            batch = ORDER[2 * b : 2 * b + 2]
            ssum = keep.tile([P, 2, V], F32, name=f"ssum{b}", tag="ssum" if b == 0 else f"placed{ORDER[0]}")
            nc.scalar.activation(ssum[:], totals[b][:], ACT.Copy, bias=0.25)
            if b == 0:
                convert_w2()
            for i, t in enumerate(batch):
                placed[t] = keep.tile([P, S], F32, name=f"placed{t}", tag=f"placed{t}")
                nc.vector.tensor_tensor(placed[t][:].indirect(lb_sb[:]), prods[b][:, i, :], invs[b][:, i, :], ALU.mult)
            for i, t in enumerate(batch):
                nc.vector.tensor_tensor(placed[t][:].indirect(la_sb[:]), ssum[:, i, :], invs[b][:, i, :], ALU.mult)
                if t != ORDER[-1]:
                    for q in range(4):
                        nc.scalar.activation(z_bf[q][:, :, t], placed[t][:, q * P : (q + 1) * P], ACT.Copy, scale=gain[:, t : t + 1])

        last = ORDER[-1]

        def round_last(q):
            nc.vector.tensor_scalar(z_bf[q][:, :, last], placed[last][:, q * P : (q + 1) * P], gain[:, last : last + 1], None, ALU.mult)

        def project(q):
            z_codes = keep.tile([P, P], U32, name=f"z_codes{q}", align_bytes=64)
            z_plane = keep.tile([P, P], U8, name=f"z_plane{q}", align_bytes=64)
            nc.vector.quantize_mx(out=z_codes[:].bitcast(FP8X4), scales=z_plane[:], in_=z_bf[q][:].rearrange("p c j -> p (c j)"))
            groups = ((0, 4),) if q in (1, 2) else ((0, 2), (2, 4))
            for lo, hi in groups:
                acc = psum.tile([P, hi - lo, P], F32, name="acc", tag="acc")
                for a in range(lo, hi):
                    m = slice(a * P, (a + 1) * P)
                    nc.tensor.matmul_mx(out=acc[:, a - lo, :], lhsT=w2_codes[:, m].bitcast(FP8X4), lhsT_scale=w2_plane[:, m], rhs=z_codes[:].bitcast(FP8X4), rhs_scale=z_plane[:], start=True, stop=True)
                res = keep.tile([P, hi - lo, P], F32, name=f"res{q}{lo}")
                if q == 2 or (q == 3 and lo == 2):
                    nc.vector.tensor_copy(res[:], acc[:])
                else:
                    nc.scalar.copy(res[:], acc[:])
                rows = out[lo * P : hi * P, q * P : (q + 1) * P].rearrange("(a p) c -> p a c", p=P)
                nc.sync.dma_start(rows, res[:])

        round_last(0)
        for q in range(4):
            if q < 3:
                round_last(q + 1)
            project(q)
